import numpy as np
import ml_dtypes


def mxq(x, axis, fmt="e4m3"):
    dtype, down = {"e4m3": (ml_dtypes.float8_e4m3fn, 7), "e5m2": (ml_dtypes.float8_e5m2, 14)}[fmt]
    v = np.moveaxis(np.asarray(x, np.float32).astype(ml_dtypes.bfloat16).astype(np.float64), axis, -1)
    blocks = v.reshape(v.shape[:-1] + (-1, 32))
    amax = np.abs(blocks).max(-1, keepdims=True)
    byte = np.maximum(np.where(amax > 0, np.frexp(amax)[1] - 1 + 127, 0) - down, 1)
    scale = np.exp2(byte - 127.0)
    codes = (blocks / scale).astype(np.float32).astype(dtype).astype(np.float64)
    return np.moveaxis((codes * scale).reshape(v.shape), -1, axis)


WIDE = False


def mx_kscale(k):
    if not WIDE:
        return np.ones(k)
    levels = np.array([10, -10, 5, -5, 0])
    if k % 512:
        return np.exp2(np.random.permutation(np.resize(levels, k // 32))).repeat(32)
    a = np.empty((k // 512, 16))
    for p in range(k // 512):
        a[p, :8] = np.random.permutation(np.resize(levels, 8))
        for g in range(8):
            far = levels[np.abs(levels - a[p, g]) >= 10]
            a[p, g + 8] = far[np.random.randint(len(far))]
    return np.exp2(a.ravel()).repeat(32)


def f64(x):
    return np.asarray(x).astype(np.float64)


def striped(idx):
    return np.tile(idx.reshape(-1, 16).T, (8, 1)).astype(np.uint16)


def unstriped(offs):
    return offs[:16].T.reshape(-1).astype(np.int64)


E2M1 = np.array([0.0, 0.5, 1.0, 1.5, 2.0, 3.0, 4.0, 6.0, -0.0, -0.5, -1.0, -1.5, -2.0, -3.0, -4.0, -6.0])


def pack_weight(w, fmt):
    k, n = w.shape
    w = f64(np.asarray(w, np.float32).astype(ml_dtypes.bfloat16)).reshape(k // 32, 32, n)
    amax = np.abs(w).max(1)
    if fmt == "e4m3":
        byte = np.frexp(amax)[1] - 1 + 127 - 7
    else:
        mant, ex = np.frexp(amax / 6.0)
        byte = np.where(mant > 0.5, ex, ex - 1) + 127
    byte = np.clip(np.where(amax > 0, byte, 1), 1, 254)
    scaled = (w * np.exp2(127.0 - byte)[:, None, :]).reshape(k, n).astype(np.float32)
    by_word = np.ascontiguousarray(scaled.reshape(k // 512, 128, 4, n).transpose(0, 1, 3, 2))
    if fmt == "e4m3":
        words = by_word.astype(ml_dtypes.float8_e4m3fn).view(np.uint8)
    else:
        c = by_word.astype(ml_dtypes.float4_e2m1fn).view(np.uint8) & 0xF
        words = (c[..., 0::2] | (c[..., 1::2] << 4)).reshape(k // 512, 128, 2 * n)
    return np.ascontiguousarray(words), np.ascontiguousarray(byte.astype(np.uint8).reshape(k // 512, 16, n))


def unpack_weight(words, scales, fmt):
    g, _, n = scales.shape
    words = np.ascontiguousarray(words).reshape(g, 128, n, -1)
    if fmt == "e4m3":
        vals = words.view(ml_dtypes.float8_e4m3fn).astype(np.float64)
    else:
        nib = np.empty((g, 128, n, 4), np.uint8)
        nib[..., 0::2] = words & 0xF
        nib[..., 1::2] = words >> 4
        vals = E2M1[nib]
    vals = vals * np.repeat(np.exp2(scales.astype(np.float64) - 127.0), 8, axis=1)[..., None]
    return vals.transpose(0, 1, 3, 2).reshape(g * 512, n)


def gelu(v):
    return 0.5 * v * (1.0 + np.tanh(np.sqrt(2.0 / np.pi) * (v + 0.044715 * v**3)))


def bf(x):
    return np.asarray(x, np.float32).astype(ml_dtypes.bfloat16)

def planes(Y):
    n, m = Y.shape
    b = f64(bf(Y)).reshape(n // 32, 32, m)
    amax = np.abs(b).max(1)
    byte = np.clip(np.where(amax > 0, np.frexp(amax)[1] - 1 + 127 - 7, 1), 1, 254)
    codes = (b * np.exp2(127.0 - byte)[:, None, :]).reshape(n, m).astype(np.float32).astype(ml_dtypes.float8_e4m3fn).view(np.uint8)
    words = codes.reshape(n // 512, 128, 4, m).transpose(0, 1, 3, 2)
    return np.ascontiguousarray(words), np.ascontiguousarray(byte.astype(np.uint8).reshape(n // 512, 16, m))


K, H, T, S, P = 1024, 1024, 4096, 1024, 512

def setup_inputs():
    n = np.random.standard_normal
    s = mx_kscale(K)[:, None]
    u = mx_kscale(H)[:, None]
    gain = np.exp(0.8 * n(H))
    tab_words, tab_scales = pack_weight(n((K, T)) * s, "e4m3")
    w1_words, w1_scales = pack_weight(n((K, H)) / np.sqrt(K) / s * u.T, "e2m1")
    w2 = 0.7 * n((H, H)) / np.sqrt(H) / u * gain[None, :]
    lam = 0.5 * np.exp(0.3 * n(H)) * gain / u[:, 0]
    return {
        "tab_words": tab_words, "tab_scales": tab_scales,
        "offs": striped(np.random.permutation(T)[:S]),
        "w1_words": w1_words, "w1_scales": w1_scales,
        "pos1": striped(np.random.permutation(S)[:P]),
        "pos2": striped(np.random.permutation(S)[:P]),
        "w2": w2.astype(np.float32),
        "lam": lam.astype(np.float32),
    }

def reference(tab_words, tab_scales, offs, w1_words, w1_scales, pos1, pos2, w2, lam):
    v = unpack_weight(tab_words, tab_scales, "e4m3")[:, unstriped(offs)]
    w1 = unpack_weight(w1_words, w1_scales, "e2m1")
    h = w1.T @ v
    a = h[:, unstriped(pos1)]
    b = h[:, unstriped(pos2)]
    z = a + b
    central = mxq(f64(w2), 0, "e4m3").T @ mxq(z, 0, "e4m3")
    jump = np.abs(a - b)
    y = central - f64(lam)[:, None] * jump
    words, scales = planes(y)
    return y, words, scales

@@ -1,0 +1,295 @@
+from contextlib import ExitStack
+
+import concourse.mybir as mybir
+from concourse.masks import make_identity
+
+K, H, T, S, NF = 1024, 1024, 4096, 1024, 512
+FLOPS = 2 * K * H * S + 2 * H * H * NF
+
+F32 = mybir.dt.float32
+BF16 = mybir.dt.bfloat16
+I32 = mybir.dt.int32
+U32 = mybir.dt.uint32
+U16 = mybir.dt.uint16
+U8 = mybir.dt.uint8
+FP8X4 = mybir.dt.float8_e4m3fn_x4
+FP4X4 = mybir.dt.float4_e2m1fn_x4
+ALU = mybir.AluOpType
+ACT = mybir.ActivationFunctionType
+
+P = 128
+PACK = 4
+GROUP = P * PACK
+PASSES = K // GROUP
+GROUPS = H // GROUP
+BANK = 512
+CHUNK = 256
+CHUNKS = NF // CHUNK
+
+
+def tile_list_face_jump_flux_kernel(
+    tc, tab_words, tab_scales, offs, w1_words, w1_scales, pos1, pos2, w2, lam, out_0, out_1, out_2
+):
+    nc = tc.nc
+    with ExitStack() as ctx:
+        lists = ctx.enter_context(tc.tile_pool(name="lists", bufs=1))
+        keep = ctx.enter_context(tc.tile_pool(name="keep", bufs=1))
+        big = ctx.enter_context(tc.tile_pool(name="big", bufs=1))
+        ring = ctx.enter_context(tc.tile_pool(name="ring", bufs=2))
+        psum = ctx.enter_context(tc.psum_pool(name="psum", bufs=1))
+
+        idx = lists.tile([P, S // 16], U16, name="idx")
+        p1 = lists.tile([P, NF // 16], U16, name="p1")
+        p2 = lists.tile([P, NF // 16], U16, name="p2")
+        nc.sync.dma_start(idx[:], offs)
+
+        tsc = keep.tile([P, T], U8, name="tsc", align_bytes=64)
+        nc.sync.dma_start(tsc[0:32, :].bitcast(I32), tab_scales.rearrange("a q t -> (a q) t").bitcast(I32))
+        nc.sync.dma_start(p1[:], pos1)
+
+        w1sc_raw = keep.tile([P, PASSES, H], U8, name="w1sc_raw", align_bytes=64)
+        nc.vector.memset(w1sc_raw[:].rearrange("p a n -> p (a n)").bitcast(I32), 0)
+        nc.vector.memset(tsc[32:64, :].bitcast(I32), 0)
+        nc.vector.memset(tsc[64:128, :].bitcast(I32), 0)
+        vsc = [keep.tile([P, S], U8, name=f"vsc{a}", align_bytes=64) for a in range(PASSES)]
+        for a in range(PASSES):
+            nc.vector.memset(vsc[a][:].bitcast(I32), 0)
+
+        tab = [big.tile([P, T], I32, name=f"tab{a}", offset=2048 + a * 4 * T) for a in range(PASSES)]
+        for a in range(PASSES):
+            nc.sync.dma_start(tab[a][:], tab_words[a].rearrange("p t i -> p (t i)").bitcast(I32))
+        w1_raw = [keep.tile([P, PASSES, 2 * GROUP], U8, name=f"w1_raw{b}", align_bytes=64) for b in range(GROUPS)]
+        for b in range(GROUPS):
+            nc.sync.dma_start(
+                w1_raw[b][:].bitcast(I32),
+                w1_words[:, :, 2 * GROUP * b : 2 * GROUP * (b + 1)].rearrange("a p n -> p a n").bitcast(I32),
+            )
+        nc.sync.dma_start(p2[:], pos2)
+
+        for q in range(4):
+            nc.gpsimd.dma_start(
+                w1sc_raw[32 * q : 32 * q + 4, :, :].bitcast(I32),
+                w1_scales[:, 4 * q : 4 * q + 4, :].rearrange("a r n -> r a n").bitcast(I32),
+            )
+        lam_sb = keep.tile([P, GROUPS, PACK], F32, name="lam_sb")
+        nc.scalar.dma_start(lam_sb[:], lam.rearrange("(g p t) -> p g t", p=P, t=PACK))
+        ident = keep.tile([P, P], F32, name="ident")
+        make_identity(nc, ident[:])
+        neg_lam = keep.tile([P, GROUPS, PACK], F32, name="neg_lam")
+        nc.scalar.activation(out=neg_lam[:], in_=lam_sb[:], func=ACT.Copy, scale=-1.0)
+
+        gsc = keep.tile([P, S], U8, name="gsc", align_bytes=64)
+        nc.vector.tensor_copy(gsc[:], tsc[:].indirect(idx[:]))
+        for a in range(PASSES):
+            queue = nc.scalar if a == 0 else nc.gpsimd
+            for q in range(4):
+                queue.dma_start(
+                    vsc[a][32 * q : 32 * q + 4, :].bitcast(I32),
+                    gsc[16 * a + 4 * q : 16 * a + 4 * q + 4, :].bitcast(I32),
+                )
+
+        halves = S // BANK
+        v = [[keep.tile([P, BANK], U32, name=f"v{a}{s}", align_bytes=64) for s in range(halves)] for a in range(PASSES)]
+
+        def gather_words(a):
+            for s in range(halves):
+                cols = slice(s * BANK // 16, (s + 1) * BANK // 16)
+                nc.vector.tensor_copy(v[a][s][:], tab[a][:].bitcast(U32).indirect(idx[:, cols]))
+
+        gather_words(0)
+        w1sc = big.tile([P, PASSES, H], U8, name="w1sc", align_bytes=64, offset=4 * T)
+        nc.vector.tensor_copy(
+            w1sc[:].rearrange("p a (b t m) -> p (a b) t m", t=PACK, m=P),
+            w1sc_raw[:].rearrange("p a (b m t) -> p (a b) t m", t=PACK, m=P),
+        )
+        gather_words(1)
+
+        w1 = [keep.tile([P, PASSES, 2 * GROUP], U8, name=f"w1_{b}", align_bytes=64) for b in range(GROUPS)]
+        for b in range(GROUPS):
+            nc.scalar.copy(
+                w1[b][:].bitcast(U16).rearrange("p a (t m) -> p a t m", t=PACK),
+                w1_raw[b][:].bitcast(U16).rearrange("p a (m t) -> p a t m", t=PACK),
+            )
+
+        w2_raw = {}
+        for a in range(GROUPS):
+            for g in range(GROUPS):
+                w2_raw[a, g] = big.tile([P, PACK, GROUP], F32, name=f"w2_raw{a}{g}", offset=(2 * a + g) * 4 * PACK * GROUP + 2048 * a)
+                nc.sync.dma_start(
+                    w2_raw[a, g][:],
+                    w2[GROUP * a : GROUP * (a + 1), GROUP * g : GROUP * (g + 1)].rearrange("(p j) n -> p j n", j=PACK),
+                )
+
+        h = [keep.tile([P, S], F32, name=f"h{k}") for k in range(GROUPS * PACK)]
+        for b in range(GROUPS):
+            for t in range(PACK):
+                for s in range(halves):
+                    step = (PACK * b + t) * halves + s
+                    acc = psum.tile([P, BANK], F32, name=f"acc{step}", offset=2048 * (step % 8))
+                    for a in range(PASSES):
+                        nc.tensor.matmul_mx(
+                            out=acc[:],
+                            lhsT=w1[b][:, a, 2 * P * t : 2 * P * (t + 1)].bitcast(FP4X4),
+                            lhsT_scale=w1sc[:, a, GROUP * b + P * t : GROUP * b + P * (t + 1)],
+                            rhs=v[a][s][:].bitcast(FP8X4),
+                            rhs_scale=vsc[a][:, BANK * s : BANK * (s + 1)],
+                            start=(a == 0),
+                            stop=(a == PASSES - 1),
+                        )
+                    nc.scalar.copy(h[PACK * b + t][:, BANK * s : BANK * (s + 1)], acc[:])
+
+        w2q = {}
+        w2sc = {}
+
+        def round_w2(a, g):
+            w2_bf = keep.tile([P, PACK * GROUP], BF16, name=f"w2_bf{a}{g}", tag=f"stage{a}{g}", align_bytes=64)
+            for t in range(PACK):
+                nc.gpsimd.tensor_scalar(
+                    w2_bf[:, GROUP * t : GROUP * (t + 1)].rearrange("p (m j) -> p m j", j=PACK),
+                    w2_raw[a, g][:].rearrange("p j (m t) -> p t m j", t=PACK)[:, t],
+                    1.0, 0.0, ALU.mult, ALU.add,
+                )
+            return w2_bf
+
+        def quantise_w2(a, g, w2_bf):
+            w2q[a, g] = keep.tile([P, GROUP], U32, name=f"w2q{a}{g}", align_bytes=64)
+            w2sc[a, g] = keep.tile([P, GROUP], U8, name=f"w2sc{a}{g}", align_bytes=64)
+            nc.vector.quantize_mx(out=w2q[a, g][:].bitcast(FP8X4), scales=w2sc[a, g][:], in_=w2_bf[:])
+
+        def pick(b, f0, width):
+            last = b == 1 and f0 > 0
+            side1 = keep.tile([P, PACK, width], F32, name=f"side1_{b}_{f0}", tag="stage10" if last else f"side1_{b}", align_bytes=64)
+            side2 = keep.tile([P, PACK, width], F32, name=f"side2_{b}_{f0}", tag="stage11" if last else f"side2_{b}", align_bytes=64)
+            cols = slice(f0 // 16, (f0 + width) // 16)
+            for t in range(PACK):
+                nc.vector.tensor_copy(side1[:, t, :], h[PACK * b + t][:].indirect(p1[:, cols]))
+                nc.vector.tensor_copy(side2[:, t, :], h[PACK * b + t][:].indirect(p2[:, cols]))
+            return side1, side2
+
+        jump = {}
+
+        def jumps(b, f0, width, sides):
+            tile_j = keep.tile([P, PACK, width], F32, name=f"jump_{b}_{f0}")
+            per = BANK // width
+            for t in range(0, PACK, per):
+                nc.gpsimd.tensor_tensor(
+                    tile_j[:, t : t + per, :], sides[0][:, t : t + per, :], sides[1][:, t : t + per, :], ALU.subtract
+                )
+            for c0 in range(0, width, CHUNK):
+                jump[b, (f0 + c0) // CHUNK] = tile_j[:, :, c0 : c0 + CHUNK]
+            return tile_j
+
+        def magnitude(tile_j):
+            per = BANK // tile_j.shape[2]
+            for t in range(0, PACK, per):
+                nc.scalar.activation(out=tile_j[:, t : t + per, :], in_=tile_j[:, t : t + per, :], func=ACT.Abs)
+
+        z_bf = {}
+
+        def sums(b, c, sides, c0):
+            back = psum.tile([P, CHUNK // P, 2, P], F32, name=f"back{b}{c}", offset=2048 * (4 + c))
+            for fb in range(CHUNK // P):
+                cols = slice(c0 + fb * P, c0 + (fb + 1) * P)
+                zt = psum.tile([P, PACK, P], F32, name=f"zt{b}{c}{fb}", offset=2048 * (6 + fb))
+                for t in range(PACK):
+                    for side in range(2):
+                        nc.tensor.matmul(
+                            zt[:, t, :], lhsT=sides[side][:, t, cols], rhs=ident[:],
+                            is_transpose=True, start=(side == 0), stop=(side == 1),
+                        )
+                zt_bf = ring.tile([P, 2, P, 2], BF16, name="zt_bf")
+                nc.scalar.copy(zt_bf[:], zt[:].rearrange("f (u e) p -> f u p e", e=2))
+                words = zt_bf[:].rearrange("f u p e -> f (u p e)").bitcast(F32)
+                for u in range(2):
+                    nc.tensor.transpose(back[:, fb, u, :], words[:, u * P : (u + 1) * P], ident[:])
+            z_bf[b, c] = keep.tile([P, CHUNK * PACK], BF16, name=f"z_bf{b}{c}", align_bytes=64)
+            nc.scalar.copy(
+                z_bf[b, c][:].bitcast(F32).rearrange("p (fb f u) -> p fb f u", u=2, f=P),
+                back[:].rearrange("p fb u f -> p fb f u"),
+            )
+
+        zq = {}
+        zsc = {}
+
+        def quantise_z(b, c):
+            zq[b, c] = keep.tile([P, CHUNK], U32, name=f"zq{b}{c}", align_bytes=64)
+            zsc[b, c] = keep.tile([P, CHUNK], U8, name=f"zsc{b}{c}", align_bytes=64)
+            nc.vector.quantize_mx(out=zq[b, c][:].bitcast(FP8X4), scales=zsc[b, c][:], in_=z_bf[b, c][:])
+
+        y = {}
+        y_bf = {}
+        ysc = keep.tile([P, GROUPS, NF], U8, name="ysc", align_bytes=64)
+        out_rows = out_0.rearrange("(g p t) f -> g p t f", p=P, t=PACK)
+
+        def fluxes(g, c):
+            y[g, c] = keep.tile([P, PACK, CHUNK], F32, name=f"y{g}{c}")
+            per = BANK // CHUNK
+            for t0 in range(0, PACK, per):
+                acc = psum.tile([P, per, CHUNK], F32, name=f"flux{g}{c}{t0}", offset=2048 * (4 * c + 2 * g + t0 // per))
+                for i in range(per):
+                    cols = slice(P * (t0 + i), P * (t0 + i + 1))
+                    for a in reversed(range(GROUPS)):
+                        nc.tensor.matmul_mx(
+                            out=acc[:, i, :],
+                            lhsT=w2q[a, g][:, cols].bitcast(FP8X4),
+                            lhsT_scale=w2sc[a, g][:, cols],
+                            rhs=zq[a, c][:].bitcast(FP8X4),
+                            rhs_scale=zsc[a, c][:],
+                            start=(a == GROUPS - 1),
+                            stop=(a == 0),
+                        )
+                for i in range(per):
+                    t = t0 + i
+                    nc.vector.scalar_tensor_tensor(
+                        y[g, c][:, t, :], jump[g, c][:, t, :], neg_lam[:, g, t : t + 1], acc[:, i, :], ALU.mult, ALU.add
+                    )
+            nc.sync.dma_start(out_rows[g, :, :, CHUNK * c : CHUNK * (c + 1)], y[g, c][:])
+            y_bf[g, c] = keep.tile([P, CHUNK * PACK], BF16, name=f"y_bf{g}{c}", align_bytes=64)
+            nc.scalar.copy(
+                y_bf[g, c][:].rearrange("p (k i t) -> p k t i", i=4, t=PACK),
+                y[g, c][:].rearrange("p t (k i) -> p k t i", i=4),
+            )
+
+        def planes(g, c):
+            yq = keep.tile([P, CHUNK], U32, name=f"yq{g}{c}", align_bytes=64)
+            nc.vector.quantize_mx(out=yq[:].bitcast(FP8X4), scales=ysc[:, g, CHUNK * c : CHUNK * (c + 1)], in_=y_bf[g, c][:])
+            nc.sync.dma_start(
+                out_1[g, :, CHUNK * c : CHUNK * (c + 1), :].rearrange("p m t -> p (m t)").bitcast(I32),
+                yq[:].bitcast(I32),
+            )
+
+        def store_scales():
+            for q in range(4):
+                nc.scalar.dma_start(
+                    out_2[:, 4 * q : 4 * q + 4, :].rearrange("g r m -> r g m").bitcast(I32),
+                    ysc[32 * q : 32 * q + 4, :, :].bitcast(I32),
+                )
+
+        w2_bf = {(a, g): round_w2(a, g) for a in range(GROUPS) for g in range(GROUPS)}
+        sides0 = pick(0, 0, NF)
+        jump0 = jumps(0, 0, NF, sides0)
+        sides10 = pick(1, 0, CHUNK)
+        jump10 = jumps(1, 0, CHUNK, sides10)
+        for a in range(GROUPS):
+            for g in range(GROUPS):
+                quantise_w2(a, g, w2_bf[a, g])
+        sides11 = pick(1, CHUNK, CHUNK)
+        jump11 = jumps(1, CHUNK, CHUNK, sides11)
+        for c in range(CHUNKS):
+            sums(0, c, sides0, CHUNK * c)
+        sums(1, 0, sides10, 0)
+        magnitude(jump0)
+        magnitude(jump10)
+        sums(1, 1, sides11, 0)
+        magnitude(jump11)
+        quantise_z(0, 0)
+        quantise_z(1, 0)
+        quantise_z(0, 1)
+        quantise_z(1, 1)
+        for c in range(CHUNKS):
+            for g in range(GROUPS):
+                fluxes(g, c)
+        for c in range(CHUNKS):
+            for g in range(GROUPS):
+                planes(g, c)
+        store_scales()

@@ -45,26 +45,27 @@ def tile_list_face_jump_flux_kernel(
 
         tsc = keep.tile([P, T], U8, name="tsc", align_bytes=64)
         nc.sync.dma_start(tsc[0:32, :].bitcast(I32), tab_scales.rearrange("a q t -> (a q) t").bitcast(I32))
-        nc.sync.dma_start(p1[:], pos1)
 
         w1sc_raw = keep.tile([P, PASSES, H], U8, name="w1sc_raw", align_bytes=64)
-        nc.vector.memset(w1sc_raw[:].rearrange("p a n -> p (a n)").bitcast(I32), 0)
+        nc.gpsimd.memset(w1sc_raw[:].rearrange("p a n -> p (a n)").bitcast(I32), 0)
         nc.vector.memset(tsc[32:64, :].bitcast(I32), 0)
         nc.vector.memset(tsc[64:128, :].bitcast(I32), 0)
         vsc = [keep.tile([P, S], U8, name=f"vsc{a}", align_bytes=64) for a in range(PASSES)]
         for a in range(PASSES):
-            nc.vector.memset(vsc[a][:].bitcast(I32), 0)
+            nc.gpsimd.memset(vsc[a][:].bitcast(I32), 0)
 
         tab = [big.tile([P, T], I32, name=f"tab{a}", offset=2048 + a * 4 * T) for a in range(PASSES)]
         for a in range(PASSES):
             nc.sync.dma_start(tab[a][:], tab_words[a].rearrange("p t i -> p (t i)").bitcast(I32))
+            if a == 0:
+                nc.sync.dma_start(p1[:], pos1)
+                nc.sync.dma_start(p2[:], pos2)
         w1_raw = [keep.tile([P, PASSES, 2 * GROUP], U8, name=f"w1_raw{b}", align_bytes=64) for b in range(GROUPS)]
         for b in range(GROUPS):
             nc.sync.dma_start(
                 w1_raw[b][:].bitcast(I32),
                 w1_words[:, :, 2 * GROUP * b : 2 * GROUP * (b + 1)].rearrange("a p n -> p a n").bitcast(I32),
             )
-        nc.sync.dma_start(p2[:], pos2)
 
         for q in range(4):
             nc.gpsimd.dma_start(
@@ -72,7 +73,7 @@ def tile_list_face_jump_flux_kernel(
                 w1_scales[:, 4 * q : 4 * q + 4, :].rearrange("a r n -> r a n").bitcast(I32),
             )
         lam_sb = keep.tile([P, GROUPS, PACK], F32, name="lam_sb")
-        nc.scalar.dma_start(lam_sb[:], lam.rearrange("(g p t) -> p g t", p=P, t=PACK))
+        nc.gpsimd.dma_start(lam_sb[:], lam.rearrange("(g p t) -> p g t", p=P, t=PACK))
         ident = keep.tile([P, P], F32, name="ident")
         make_identity(nc, ident[:])
         neg_lam = keep.tile([P, GROUPS, PACK], F32, name="neg_lam")
@@ -81,8 +82,8 @@ def tile_list_face_jump_flux_kernel(
         gsc = keep.tile([P, S], U8, name="gsc", align_bytes=64)
         nc.vector.tensor_copy(gsc[:], tsc[:].indirect(idx[:]))
         for a in range(PASSES):
-            queue = nc.scalar if a == 0 else nc.gpsimd
             for q in range(4):
+                queue = nc.scalar if 4 * a + q < 5 else nc.gpsimd
                 queue.dma_start(
                     vsc[a][32 * q : 32 * q + 4, :].bitcast(I32),
                     gsc[16 * a + 4 * q : 16 * a + 4 * q + 4, :].bitcast(I32),
@@ -143,12 +144,12 @@ def tile_list_face_jump_flux_kernel(
 
         def round_w2(a, g):
             w2_bf = keep.tile([P, PACK * GROUP], BF16, name=f"w2_bf{a}{g}", tag=f"stage{a}{g}", align_bytes=64)
-            for t in range(PACK):
-                nc.gpsimd.tensor_scalar(
-                    w2_bf[:, GROUP * t : GROUP * (t + 1)].rearrange("p (m j) -> p m j", j=PACK),
-                    w2_raw[a, g][:].rearrange("p j (m t) -> p t m j", t=PACK)[:, t],
-                    1.0, 0.0, ALU.mult, ALU.add,
-                )
+            dst = w2_bf[:].rearrange("p (t m j) -> p m j t", t=PACK, j=PACK)
+            src = w2_raw[a, g][:].rearrange("p j (m t) -> p m j t", t=PACK)
+            if (a, g) in ():
+                nc.vector.tensor_copy(dst, src)
+            else:
+                nc.scalar.copy(dst, src)
             return w2_bf
 
         def quantise_w2(a, g, w2_bf):
@@ -158,8 +159,8 @@ def tile_list_face_jump_flux_kernel(
 
         def pick(b, f0, width):
             last = b == 1 and f0 > 0
-            side1 = keep.tile([P, PACK, width], F32, name=f"side1_{b}_{f0}", tag="stage10" if last else f"side1_{b}", align_bytes=64)
-            side2 = keep.tile([P, PACK, width], F32, name=f"side2_{b}_{f0}", tag="stage11" if last else f"side2_{b}", align_bytes=64)
+            side1 = keep.tile([P, PACK, width], F32, name=f"side1_{b}_{f0}", tag="stage11" if last else f"side1_{b}", align_bytes=64)
+            side2 = keep.tile([P, PACK, width], F32, name=f"side2_{b}_{f0}", tag="zstage10" if last else f"side2_{b}", align_bytes=64)
             cols = slice(f0 // 16, (f0 + width) // 16)
             for t in range(PACK):
                 nc.vector.tensor_copy(side1[:, t, :], h[PACK * b + t][:].indirect(p1[:, cols]))
@@ -170,11 +171,7 @@ def tile_list_face_jump_flux_kernel(
 
         def jumps(b, f0, width, sides):
             tile_j = keep.tile([P, PACK, width], F32, name=f"jump_{b}_{f0}")
-            per = BANK // width
-            for t in range(0, PACK, per):
-                nc.gpsimd.tensor_tensor(
-                    tile_j[:, t : t + per, :], sides[0][:, t : t + per, :], sides[1][:, t : t + per, :], ALU.subtract
-                )
+            nc.vector.tensor_tensor(tile_j[:], sides[0][:], sides[1][:], ALU.subtract)
             for c0 in range(0, width, CHUNK):
                 jump[b, (f0 + c0) // CHUNK] = tile_j[:, :, c0 : c0 + CHUNK]
             return tile_j
@@ -202,7 +199,7 @@ def tile_list_face_jump_flux_kernel(
                 words = zt_bf[:].rearrange("f u p e -> f (u p e)").bitcast(F32)
                 for u in range(2):
                     nc.tensor.transpose(back[:, fb, u, :], words[:, u * P : (u + 1) * P], ident[:])
-            z_bf[b, c] = keep.tile([P, CHUNK * PACK], BF16, name=f"z_bf{b}{c}", align_bytes=64)
+            z_bf[b, c] = keep.tile([P, CHUNK * PACK], BF16, name=f"z_bf{b}{c}", tag=f"zstage{b}{c}", align_bytes=64)
             nc.scalar.copy(
                 z_bf[b, c][:].bitcast(F32).rearrange("p (fb f u) -> p fb f u", u=2, f=P),
                 back[:].rearrange("p fb u f -> p fb f u"),
@@ -245,16 +242,20 @@ def tile_list_face_jump_flux_kernel(
                     )
             nc.sync.dma_start(out_rows[g, :, :, CHUNK * c : CHUNK * (c + 1)], y[g, c][:])
             y_bf[g, c] = keep.tile([P, CHUNK * PACK], BF16, name=f"y_bf{g}{c}", align_bytes=64)
-            nc.scalar.copy(
+            rounder = nc.vector.tensor_copy if (g, c) in () else nc.scalar.copy
+            rounder(
                 y_bf[g, c][:].rearrange("p (k i t) -> p k t i", i=4, t=PACK),
                 y[g, c][:].rearrange("p t (k i) -> p k t i", i=4),
             )
 
-        def planes(g, c):
-            yq = keep.tile([P, CHUNK], U32, name=f"yq{g}{c}", align_bytes=64)
-            nc.vector.quantize_mx(out=yq[:].bitcast(FP8X4), scales=ysc[:, g, CHUNK * c : CHUNK * (c + 1)], in_=y_bf[g, c][:])
+        def planes(c):
+            yq = keep.tile([P, GROUPS, CHUNK], U32, name=f"yq{c}", align_bytes=64)
+            for g in range(GROUPS):
+                nc.vector.quantize_mx(
+                    out=yq[:, g, :].bitcast(FP8X4), scales=ysc[:, g, CHUNK * c : CHUNK * (c + 1)], in_=y_bf[g, c][:]
+                )
             nc.sync.dma_start(
-                out_1[g, :, CHUNK * c : CHUNK * (c + 1), :].rearrange("p m t -> p (m t)").bitcast(I32),
+                out_1[:, :, CHUNK * c : CHUNK * (c + 1), :].rearrange("g p m t -> p g (m t)").bitcast(I32),
                 yq[:].bitcast(I32),
             )
 
@@ -273,23 +274,22 @@ def tile_list_face_jump_flux_kernel(
         for a in range(GROUPS):
             for g in range(GROUPS):
                 quantise_w2(a, g, w2_bf[a, g])
+        sums(0, 0, sides0, 0)
+        sums(1, 0, sides10, 0)
+        quantise_z(0, 0)
+        quantise_z(1, 0)
         sides11 = pick(1, CHUNK, CHUNK)
         jump11 = jumps(1, CHUNK, CHUNK, sides11)
-        for c in range(CHUNKS):
-            sums(0, c, sides0, CHUNK * c)
-        sums(1, 0, sides10, 0)
+        sums(0, 1, sides0, CHUNK)
         magnitude(jump0)
         magnitude(jump10)
         sums(1, 1, sides11, 0)
         magnitude(jump11)
-        quantise_z(0, 0)
-        quantise_z(1, 0)
         quantise_z(0, 1)
         quantise_z(1, 1)
         for c in range(CHUNKS):
             for g in range(GROUPS):
                 fluxes(g, c)
         for c in range(CHUNKS):
-            for g in range(GROUPS):
-                planes(g, c)
+            planes(c)
         store_scales()

@@ -25,6 +25,13 @@ GROUPS = H // GROUP
 BANK = 512
 CHUNK = 256
 CHUNKS = NF // CHUNK
+BANKS = {(0, 0): 0, (1, 0): 2, (0, 1): 4, (1, 1): 6}
+SUM_BANKS = {(0, 0): (6, 0), (1, 0): (4, 1), (0, 1): (6, 4)}
+KIB = 1024
+TAB0 = 0
+GSC = 24 * KIB
+TAB1 = 31 * KIB
+W2_RAW = {(0, 0): GSC + 256 - 8 * KIB, (0, 1): TAB1 - 4 * KIB, (1, 0): TAB1 + 4 * KIB, (1, 1): TAB1 + 13 * KIB}
 
 
 def tile_list_face_jump_flux_kernel(
@@ -43,51 +50,61 @@ def tile_list_face_jump_flux_kernel(
         p2 = lists.tile([P, NF // 16], U16, name="p2")
         nc.sync.dma_start(idx[:], offs)
 
-        tsc = keep.tile([P, T], U8, name="tsc", align_bytes=64)
+        tsc = big.tile([P, T], U8, name="tsc", align_bytes=64, offset=TAB1)
         nc.sync.dma_start(tsc[0:32, :].bitcast(I32), tab_scales.rearrange("a q t -> (a q) t").bitcast(I32))
 
         w1sc_raw = keep.tile([P, PASSES, H], U8, name="w1sc_raw", align_bytes=64)
-        nc.gpsimd.memset(w1sc_raw[:].rearrange("p a n -> p (a n)").bitcast(I32), 0)
+        nc.vector.memset(w1sc_raw[:].rearrange("p a n -> p (a n)").bitcast(I32), 0)
         nc.vector.memset(tsc[32:64, :].bitcast(I32), 0)
         nc.vector.memset(tsc[64:128, :].bitcast(I32), 0)
         vsc = [keep.tile([P, S], U8, name=f"vsc{a}", align_bytes=64) for a in range(PASSES)]
         for a in range(PASSES):
-            nc.gpsimd.memset(vsc[a][:].bitcast(I32), 0)
+            nc.vector.memset(vsc[a][:].bitcast(I32), 0)
 
-        tab = [big.tile([P, T], I32, name=f"tab{a}", offset=2048 + a * 4 * T) for a in range(PASSES)]
-        for a in range(PASSES):
+        tab = [big.tile([P, T], I32, name=f"tab{a}", offset=(TAB0, TAB1)[a]) for a in range(PASSES)]
+
+        def load_words(a):
             nc.sync.dma_start(tab[a][:], tab_words[a].rearrange("p t i -> p (t i)").bitcast(I32))
-            if a == 0:
-                nc.sync.dma_start(p1[:], pos1)
-                nc.sync.dma_start(p2[:], pos2)
-        w1_raw = [keep.tile([P, PASSES, 2 * GROUP], U8, name=f"w1_raw{b}", align_bytes=64) for b in range(GROUPS)]
-        for b in range(GROUPS):
+
+        w1_raw = [
+            keep.tile([P, PASSES, 2 * GROUP], U8, name="w1_raw0", align_bytes=64),
+            big.tile([P, PASSES, 2 * GROUP], U8, name="w1_raw1", align_bytes=64, offset=GSC + 768),
+        ]
+
+        def load_w1(b):
             nc.sync.dma_start(
                 w1_raw[b][:].bitcast(I32),
                 w1_words[:, :, 2 * GROUP * b : 2 * GROUP * (b + 1)].rearrange("a p n -> p a n").bitcast(I32),
             )
+
+        nc.sync.dma_start(p1[:], pos1)
+        nc.sync.dma_start(p2[:], pos2)
+        lam_sb = keep.tile([P, GROUPS, PACK], F32, name="lam_sb")
+        nc.sync.dma_start(lam_sb[:], lam.rearrange("(g p t) -> p g t", p=P, t=PACK))
+        load_words(0)
+        load_w1(0)
 
         for q in range(4):
             nc.gpsimd.dma_start(
                 w1sc_raw[32 * q : 32 * q + 4, :, :].bitcast(I32),
                 w1_scales[:, 4 * q : 4 * q + 4, :].rearrange("a r n -> r a n").bitcast(I32),
             )
-        lam_sb = keep.tile([P, GROUPS, PACK], F32, name="lam_sb")
-        nc.gpsimd.dma_start(lam_sb[:], lam.rearrange("(g p t) -> p g t", p=P, t=PACK))
-        ident = keep.tile([P, P], F32, name="ident")
-        make_identity(nc, ident[:])
         neg_lam = keep.tile([P, GROUPS, PACK], F32, name="neg_lam")
         nc.scalar.activation(out=neg_lam[:], in_=lam_sb[:], func=ACT.Copy, scale=-1.0)
 
-        gsc = keep.tile([P, S], U8, name="gsc", align_bytes=64)
+        gsc = big.tile([P, S], U8, name="gsc", align_bytes=64, offset=GSC)
         nc.vector.tensor_copy(gsc[:], tsc[:].indirect(idx[:]))
+        load_words(1)
         for a in range(PASSES):
             for q in range(4):
-                queue = nc.scalar if 4 * a + q < 5 else nc.gpsimd
+                queue = nc.scalar if 4 * a + q < 7 else nc.gpsimd
                 queue.dma_start(
                     vsc[a][32 * q : 32 * q + 4, :].bitcast(I32),
                     gsc[16 * a + 4 * q : 16 * a + 4 * q + 4, :].bitcast(I32),
                 )
+
+        ident = big.tile([P, P], F32, name="ident", offset=GSC + 256)
+        make_identity(nc, ident[:])
 
         halves = S // BANK
         v = [[keep.tile([P, BANK], U32, name=f"v{a}{s}", align_bytes=64) for s in range(halves)] for a in range(PASSES)]
@@ -98,12 +115,21 @@ def tile_list_face_jump_flux_kernel(
                 nc.vector.tensor_copy(v[a][s][:], tab[a][:].bitcast(U32).indirect(idx[:, cols]))
 
         gather_words(0)
-        w1sc = big.tile([P, PASSES, H], U8, name="w1sc", align_bytes=64, offset=4 * T)
-        nc.vector.tensor_copy(
-            w1sc[:].rearrange("p a (b t m) -> p (a b) t m", t=PACK, m=P),
-            w1sc_raw[:].rearrange("p a (b m t) -> p (a b) t m", t=PACK, m=P),
-        )
+        load_w1(1)
+        w1sc = [
+            big.tile([P, PASSES, GROUP], U8, name=f"w1sc{b}", align_bytes=64, offset=(TAB0, TAB1)[b] + 12 * KIB)
+            for b in range(GROUPS)
+        ]
+
+        def deal_w1_scales(b):
+            nc.vector.tensor_copy(
+                w1sc[b][:].rearrange("p a (t m) -> p a t m", t=PACK),
+                w1sc_raw[:, :, GROUP * b : GROUP * (b + 1)].rearrange("p a (m t) -> p a t m", t=PACK),
+            )
+
+        deal_w1_scales(0)
         gather_words(1)
+        deal_w1_scales(1)
 
         w1 = [keep.tile([P, PASSES, 2 * GROUP], U8, name=f"w1_{b}", align_bytes=64) for b in range(GROUPS)]
         for b in range(GROUPS):
@@ -115,7 +141,7 @@ def tile_list_face_jump_flux_kernel(
         w2_raw = {}
         for a in range(GROUPS):
             for g in range(GROUPS):
-                w2_raw[a, g] = big.tile([P, PACK, GROUP], F32, name=f"w2_raw{a}{g}", offset=(2 * a + g) * 4 * PACK * GROUP + 2048 * a)
+                w2_raw[a, g] = big.tile([P, PACK, GROUP], F32, name=f"w2_raw{a}{g}", offset=W2_RAW[a, g])
                 nc.sync.dma_start(
                     w2_raw[a, g][:],
                     w2[GROUP * a : GROUP * (a + 1), GROUP * g : GROUP * (g + 1)].rearrange("(p j) n -> p j n", j=PACK),
@@ -123,21 +149,30 @@ def tile_list_face_jump_flux_kernel(
 
         h = [keep.tile([P, S], F32, name=f"h{k}") for k in range(GROUPS * PACK)]
         for b in range(GROUPS):
-            for t in range(PACK):
-                for s in range(halves):
-                    step = (PACK * b + t) * halves + s
-                    acc = psum.tile([P, BANK], F32, name=f"acc{step}", offset=2048 * (step % 8))
-                    for a in range(PASSES):
-                        nc.tensor.matmul_mx(
-                            out=acc[:],
-                            lhsT=w1[b][:, a, 2 * P * t : 2 * P * (t + 1)].bitcast(FP4X4),
-                            lhsT_scale=w1sc[:, a, GROUP * b + P * t : GROUP * b + P * (t + 1)],
-                            rhs=v[a][s][:].bitcast(FP8X4),
-                            rhs_scale=vsc[a][:, BANK * s : BANK * (s + 1)],
-                            start=(a == 0),
-                            stop=(a == PASSES - 1),
-                        )
-                    nc.scalar.copy(h[PACK * b + t][:, BANK * s : BANK * (s + 1)], acc[:])
+            steps = [(t, s) for t in range(PACK) for s in range(halves)]
+            acc = {
+                (t, s): psum.tile([P, BANK], F32, name=f"acc{b}{t}{s}", offset=2048 * (halves * t + s)) for t, s in steps
+            }
+
+            def states(t, s, a):
+                nc.tensor.matmul_mx(
+                    out=acc[t, s][:],
+                    lhsT=w1[b][:, a, 2 * P * t : 2 * P * (t + 1)].bitcast(FP4X4),
+                    lhsT_scale=w1sc[b][:, a, P * t : P * (t + 1)],
+                    rhs=v[a][s][:].bitcast(FP8X4),
+                    rhs_scale=vsc[a][:, BANK * s : BANK * (s + 1)],
+                    start=(a == 0),
+                    stop=(a == PASSES - 1),
+                )
+
+            if b == 0:
+                for t, s in steps:
+                    states(t, s, 0)
+            for t, s in steps:
+                if b > 0:
+                    states(t, s, 0)
+                states(t, s, 1)
+                nc.scalar.copy(h[PACK * b + t][:, BANK * s : BANK * (s + 1)], acc[t, s][:])
 
         w2q = {}
         w2sc = {}
@@ -183,26 +218,43 @@ def tile_list_face_jump_flux_kernel(
 
         z_bf = {}
 
-        def sums(b, c, sides, c0):
-            back = psum.tile([P, CHUNK // P, 2, P], F32, name=f"back{b}{c}", offset=2048 * (4 + c))
-            for fb in range(CHUNK // P):
-                cols = slice(c0 + fb * P, c0 + (fb + 1) * P)
-                zt = psum.tile([P, PACK, P], F32, name=f"zt{b}{c}{fb}", offset=2048 * (6 + fb))
-                for t in range(PACK):
+        back = {}
+
+        def new_z(b, c):
+            z_bf[b, c] = keep.tile([P, CHUNK * PACK], BF16, name=f"z_bf{b}{c}", tag=f"zstage{b}{c}", align_bytes=64)
+            return z_bf[b, c]
+
+        def sums_turned(b, c, sides, c0):
+            blocks = range(CHUNK // P)
+            zt_bank, back_bank = SUM_BANKS[b, c]
+            zt = [psum.tile([P, PACK, P], F32, name=f"zt{b}{c}{fb}", offset=2048 * (zt_bank + fb)) for fb in blocks]
+            for t in range(PACK):
+                for fb in blocks:
                     for side in range(2):
                         nc.tensor.matmul(
-                            zt[:, t, :], lhsT=sides[side][:, t, cols], rhs=ident[:],
+                            zt[fb][:, t, :], lhsT=sides[side][:, t, c0 + fb * P : c0 + (fb + 1) * P], rhs=ident[:],
                             is_transpose=True, start=(side == 0), stop=(side == 1),
                         )
-                zt_bf = ring.tile([P, 2, P, 2], BF16, name="zt_bf")
-                nc.scalar.copy(zt_bf[:], zt[:].rearrange("f (u e) p -> f u p e", e=2))
+            back[b, c] = psum.tile([P, CHUNK // P, 2, P], F32, name=f"back{b}{c}", offset=2048 * back_bank)
+            for fb in blocks:
+                zt_bf = keep.tile([P, 2, P, 2], BF16, name=f"zt_bf{b}{c}{fb}")
+                nc.scalar.copy(zt_bf[:], zt[fb][:].rearrange("f (u e) p -> f u p e", e=2))
                 words = zt_bf[:].rearrange("f u p e -> f (u p e)").bitcast(F32)
                 for u in range(2):
-                    nc.tensor.transpose(back[:, fb, u, :], words[:, u * P : (u + 1) * P], ident[:])
-            z_bf[b, c] = keep.tile([P, CHUNK * PACK], BF16, name=f"z_bf{b}{c}", tag=f"zstage{b}{c}", align_bytes=64)
+                    nc.tensor.transpose(back[b, c][:, fb, u, :], words[:, u * P : (u + 1) * P], ident[:])
+
+        def sums_back(b, c):
             nc.scalar.copy(
-                z_bf[b, c][:].bitcast(F32).rearrange("p (fb f u) -> p fb f u", u=2, f=P),
-                back[:].rearrange("p fb u f -> p fb f u"),
+                new_z(b, c)[:].bitcast(F32).rearrange("p (fb f u) -> p fb f u", u=2, f=P),
+                back[b, c][:].rearrange("p fb u f -> p fb f u"),
+            )
+
+        def sums_direct(b, c, sides):
+            nc.vector.tensor_tensor(
+                new_z(b, c)[:].rearrange("p (k i t) -> p k t i", i=2, t=PACK),
+                sides[0][:].rearrange("p t (k i) -> p k t i", i=2),
+                sides[1][:].rearrange("p t (k i) -> p k t i", i=2),
+                ALU.add,
             )
 
         zq = {}
@@ -218,13 +270,16 @@ def tile_list_face_jump_flux_kernel(
         ysc = keep.tile([P, GROUPS, NF], U8, name="ysc", align_bytes=64)
         out_rows = out_0.rearrange("(g p t) f -> g p t f", p=P, t=PACK)
 
-        def fluxes(g, c):
-            y[g, c] = keep.tile([P, PACK, CHUNK], F32, name=f"y{g}{c}")
+        central = {}
+
+        def products(g, c):
             per = BANK // CHUNK
             for t0 in range(0, PACK, per):
-                acc = psum.tile([P, per, CHUNK], F32, name=f"flux{g}{c}{t0}", offset=2048 * (4 * c + 2 * g + t0 // per))
+                bank = BANKS[g, c] + t0 // per
+                acc = psum.tile([P, per, CHUNK], F32, name=f"central{g}{c}{t0}", offset=2048 * bank)
                 for i in range(per):
                     cols = slice(P * (t0 + i), P * (t0 + i + 1))
+                    central[g, c, t0 + i] = acc[:, i, :]
                     for a in reversed(range(GROUPS)):
                         nc.tensor.matmul_mx(
                             out=acc[:, i, :],
@@ -235,15 +290,21 @@ def tile_list_face_jump_flux_kernel(
                             start=(a == GROUPS - 1),
                             stop=(a == 0),
                         )
-                for i in range(per):
-                    t = t0 + i
-                    nc.vector.scalar_tensor_tensor(
-                        y[g, c][:, t, :], jump[g, c][:, t, :], neg_lam[:, g, t : t + 1], acc[:, i, :], ALU.mult, ALU.add
-                    )
+
+        def fluxes(g, c):
+            if (g, c) == (1, 1):
+                y[g, c] = keep.tile([P, PACK, CHUNK], F32, name=f"y{g}{c}")
+            else:
+                y[g, c] = big.tile([P, PACK, CHUNK], F32, name=f"y{g}{c}", offset=TAB0 + 4 * KIB * (2 * c + g))
+            for t in range(PACK):
+                nc.vector.scalar_tensor_tensor(
+                    y[g, c][:, t, :], jump[g, c][:, t, :], neg_lam[:, g, t : t + 1], central[g, c, t], ALU.mult, ALU.add
+                )
             nc.sync.dma_start(out_rows[g, :, :, CHUNK * c : CHUNK * (c + 1)], y[g, c][:])
+
+        def round_y(g, c):
             y_bf[g, c] = keep.tile([P, CHUNK * PACK], BF16, name=f"y_bf{g}{c}", align_bytes=64)
-            rounder = nc.vector.tensor_copy if (g, c) in () else nc.scalar.copy
-            rounder(
+            nc.scalar.copy(
                 y_bf[g, c][:].rearrange("p (k i t) -> p k t i", i=4, t=PACK),
                 y[g, c][:].rearrange("p t (k i) -> p k t i", i=4),
             )
@@ -274,22 +335,29 @@ def tile_list_face_jump_flux_kernel(
         for a in range(GROUPS):
             for g in range(GROUPS):
                 quantise_w2(a, g, w2_bf[a, g])
-        sums(0, 0, sides0, 0)
-        sums(1, 0, sides10, 0)
-        quantise_z(0, 0)
-        quantise_z(1, 0)
-        sides11 = pick(1, CHUNK, CHUNK)
-        jump11 = jumps(1, CHUNK, CHUNK, sides11)
-        sums(0, 1, sides0, CHUNK)
+        sums_turned(0, 0, sides0, 0)
+        sums_turned(1, 0, sides10, 0)
+        for b in range(GROUPS):
+            sums_back(b, 0)
+            quantise_z(b, 0)
+        sums_turned(0, 1, sides0, CHUNK)
+        sums_back(0, 1)
+        for g in range(GROUPS):
+            products(g, 0)
         magnitude(jump0)
         magnitude(jump10)
-        sums(1, 1, sides11, 0)
-        magnitude(jump11)
+        sides11 = pick(1, CHUNK, CHUNK)
+        sums_direct(1, 1, sides11)
         quantise_z(0, 1)
         quantise_z(1, 1)
+        for g in range(GROUPS):
+            products(g, 1)
+        jump11 = jumps(1, CHUNK, CHUNK, sides11)
+        magnitude(jump11)
         for c in range(CHUNKS):
             for g in range(GROUPS):
                 fluxes(g, c)
+                round_y(g, c)
         for c in range(CHUNKS):
             planes(c)
         store_scales()

@@ -25,13 +25,16 @@ GROUPS = H // GROUP
 BANK = 512
 CHUNK = 256
 CHUNKS = NF // CHUNK
-BANKS = {(0, 0): 0, (1, 0): 2, (0, 1): 4, (1, 1): 6}
-SUM_BANKS = {(0, 0): (6, 0), (1, 0): (4, 1), (0, 1): (6, 4)}
+BANKS = {(0, 0): 2, (1, 0): 6, (0, 1): 0, (1, 1): 4}
+SUM_BANKS = {(0, 0): (0, 6), (1, 0): (2, 7), (0, 1): (0, 4)}
+RUNS = ((0, 512), (512, 1024))
+LAST_RUNS = ((0, 512), (512, 768), (768, 1024))
 KIB = 1024
 TAB0 = 0
 GSC = 24 * KIB
-TAB1 = 31 * KIB
-W2_RAW = {(0, 0): GSC + 256 - 8 * KIB, (0, 1): TAB1 - 4 * KIB, (1, 0): TAB1 + 4 * KIB, (1, 1): TAB1 + 13 * KIB}
+TAB1 = 35 * KIB
+PICKED = 52 * KIB
+W2_RAW = {(0, 0): GSC + 256 - 8 * KIB, (0, 1): GSC + 768, (1, 0): TAB1, (1, 1): TAB1 + 9 * KIB}
 
 
 def tile_list_face_jump_flux_kernel(
@@ -50,7 +53,7 @@ def tile_list_face_jump_flux_kernel(
         p2 = lists.tile([P, NF // 16], U16, name="p2")
         nc.sync.dma_start(idx[:], offs)
 
-        tsc = big.tile([P, T], U8, name="tsc", align_bytes=64, offset=TAB1)
+        tsc = big.tile([P, T], U8, name="tsc", align_bytes=64, offset=TAB1 - 2 * KIB)
         nc.sync.dma_start(tsc[0:32, :].bitcast(I32), tab_scales.rearrange("a q t -> (a q) t").bitcast(I32))
 
         w1sc_raw = keep.tile([P, PASSES, H], U8, name="w1sc_raw", align_bytes=64)
@@ -68,7 +71,7 @@ def tile_list_face_jump_flux_kernel(
 
         w1_raw = [
             keep.tile([P, PASSES, 2 * GROUP], U8, name="w1_raw0", align_bytes=64),
-            big.tile([P, PASSES, 2 * GROUP], U8, name="w1_raw1", align_bytes=64, offset=GSC + 768),
+            big.tile([P, PASSES, 2 * GROUP], U8, name="w1_raw1", align_bytes=64, offset=TAB1 - 2 * KIB),
         ]
 
         def load_w1(b):
@@ -95,9 +98,10 @@ def tile_list_face_jump_flux_kernel(
         gsc = big.tile([P, S], U8, name="gsc", align_bytes=64, offset=GSC)
         nc.vector.tensor_copy(gsc[:], tsc[:].indirect(idx[:]))
         load_words(1)
+        load_w1(1)
         for a in range(PASSES):
             for q in range(4):
-                queue = nc.scalar if 4 * a + q < 7 else nc.gpsimd
+                queue = nc.scalar if 4 * a + q < 6 else nc.gpsimd
                 queue.dma_start(
                     vsc[a][32 * q : 32 * q + 4, :].bitcast(I32),
                     gsc[16 * a + 4 * q : 16 * a + 4 * q + 4, :].bitcast(I32),
@@ -107,29 +111,37 @@ def tile_list_face_jump_flux_kernel(
         make_identity(nc, ident[:])
 
         halves = S // BANK
-        v = [[keep.tile([P, BANK], U32, name=f"v{a}{s}", align_bytes=64) for s in range(halves)] for a in range(PASSES)]
-
-        def gather_words(a):
-            for s in range(halves):
-                cols = slice(s * BANK // 16, (s + 1) * BANK // 16)
-                nc.vector.tensor_copy(v[a][s][:], tab[a][:].bitcast(U32).indirect(idx[:, cols]))
-
-        gather_words(0)
-        load_w1(1)
-        w1sc = [
-            big.tile([P, PASSES, GROUP], U8, name=f"w1sc{b}", align_bytes=64, offset=(TAB0, TAB1)[b] + 12 * KIB)
-            for b in range(GROUPS)
+        v = [
+            [
+                big.tile([P, BANK], U32, name=f"v{a}{s}", align_bytes=64, offset=PICKED + 2 * KIB * (halves * a + s))
+                for s in range(halves)
+            ]
+            for a in range(PASSES)
         ]
 
-        def deal_w1_scales(b):
-            nc.vector.tensor_copy(
-                w1sc[b][:].rearrange("p a (t m) -> p a t m", t=PACK),
-                w1sc_raw[:, :, GROUP * b : GROUP * (b + 1)].rearrange("p a (m t) -> p a t m", t=PACK),
-            )
+        def gather_words(a):
+            for j0, j1 in (LAST_RUNS if a == PASSES - 1 else RUNS):
+                nc.vector.tensor_copy(
+                    v[a][j0 // BANK][:, j0 % BANK : j0 % BANK + j1 - j0],
+                    tab[a][:].bitcast(U32).indirect(idx[:, j0 // 16 : j1 // 16]),
+                )
 
-        deal_w1_scales(0)
-        gather_words(1)
-        deal_w1_scales(1)
+        gather_words(0)
+        w1sc = {
+            (b, a): big.tile(
+                [P, GROUP], U8, name=f"w1sc{b}{a}", align_bytes=64,
+                offset=TAB1 + 8 * KIB if (b, a) == (1, 1) else TAB0 + 12 * KIB + GROUP * (PASSES * b + a),
+            )
+            for b in range(GROUPS)
+            for a in range(PASSES)
+        }
+        for (b, a), dealt in w1sc.items():
+            if (b, a) == (1, 1):
+                gather_words(1)
+            nc.vector.tensor_copy(
+                dealt[:].rearrange("p (t m) -> p t m", t=PACK),
+                w1sc_raw[:, a, GROUP * b : GROUP * (b + 1)].rearrange("p (m t) -> p t m", t=PACK),
+            )
 
         w1 = [keep.tile([P, PASSES, 2 * GROUP], U8, name=f"w1_{b}", align_bytes=64) for b in range(GROUPS)]
         for b in range(GROUPS):
@@ -148,31 +160,35 @@ def tile_list_face_jump_flux_kernel(
                 )
 
         h = [keep.tile([P, S], F32, name=f"h{k}") for k in range(GROUPS * PACK)]
-        for b in range(GROUPS):
-            steps = [(t, s) for t in range(PACK) for s in range(halves)]
-            acc = {
-                (t, s): psum.tile([P, BANK], F32, name=f"acc{b}{t}{s}", offset=2048 * (halves * t + s)) for t, s in steps
-            }
+        steps = [
+            (k, j0, j1) for k in range(GROUPS * PACK) for j0, j1 in (LAST_RUNS if k == 0 else RUNS)
+        ]
+        acc = {}
+        for k, j0, j1 in steps:
+            bank = 6 if (k, j0) == (0, 768) else (halves * k + j0 // BANK) % 6
+            acc[k, j0] = psum.tile([P, j1 - j0], F32, name=f"acc{k}_{j0}", offset=2048 * bank)
 
-            def states(t, s, a):
-                nc.tensor.matmul_mx(
-                    out=acc[t, s][:],
-                    lhsT=w1[b][:, a, 2 * P * t : 2 * P * (t + 1)].bitcast(FP4X4),
-                    lhsT_scale=w1sc[b][:, a, P * t : P * (t + 1)],
-                    rhs=v[a][s][:].bitcast(FP8X4),
-                    rhs_scale=vsc[a][:, BANK * s : BANK * (s + 1)],
-                    start=(a == 0),
-                    stop=(a == PASSES - 1),
-                )
+        def states(k, j0, j1, a):
+            b, t = divmod(k, PACK)
+            nc.tensor.matmul_mx(
+                out=acc[k, j0][:],
+                lhsT=w1[b][:, a, 2 * P * t : 2 * P * (t + 1)].bitcast(FP4X4),
+                lhsT_scale=w1sc[b, a][:, P * t : P * (t + 1)],
+                rhs=v[a][j0 // BANK][:, j0 % BANK : j0 % BANK + j1 - j0].bitcast(FP8X4),
+                rhs_scale=vsc[a][:, j0:j1],
+                start=(a == 0),
+                stop=(a == PASSES - 1),
+            )
 
-            if b == 0:
-                for t, s in steps:
-                    states(t, s, 0)
-            for t, s in steps:
-                if b > 0:
-                    states(t, s, 0)
-                states(t, s, 1)
-                nc.scalar.copy(h[PACK * b + t][:, BANK * s : BANK * (s + 1)], acc[t, s][:])
+        early = [step for step in steps if step[0] < 3]
+        for step in early:
+            states(*step, 0)
+        for step in steps:
+            k, j0, j1 = step
+            if step not in early:
+                states(*step, 0)
+            states(*step, 1)
+            nc.scalar.copy(h[k][:, j0:j1], acc[k, j0][:])
 
         w2q = {}
         w2sc = {}
@@ -205,7 +221,10 @@ def tile_list_face_jump_flux_kernel(
         jump = {}
 
         def jumps(b, f0, width, sides):
-            tile_j = keep.tile([P, PACK, width], F32, name=f"jump_{b}_{f0}")
+            if (b, f0) == (1, CHUNK):
+                tile_j = keep.tile([P, PACK, width], F32, name=f"jump_{b}_{f0}")
+            else:
+                tile_j = big.tile([P, PACK, width], F32, name=f"jump_{b}_{f0}", offset=(PICKED, W2_RAW[0, 0])[b])
             nc.vector.tensor_tensor(tile_j[:], sides[0][:], sides[1][:], ALU.subtract)
             for c0 in range(0, width, CHUNK):
                 jump[b, (f0 + c0) // CHUNK] = tile_j[:, :, c0 : c0 + CHUNK]
@@ -322,7 +341,7 @@ def tile_list_face_jump_flux_kernel(
 
         def store_scales():
             for q in range(4):
-                nc.scalar.dma_start(
+                (nc.scalar, nc.sync)[q % 2].dma_start(
                     out_2[:, 4 * q : 4 * q + 4, :].rearrange("g r m -> r g m").bitcast(I32),
                     ysc[32 * q : 32 * q + 4, :, :].bitcast(I32),
                 )
@@ -331,10 +350,10 @@ def tile_list_face_jump_flux_kernel(
         sides0 = pick(0, 0, NF)
         jump0 = jumps(0, 0, NF, sides0)
         sides10 = pick(1, 0, CHUNK)
-        jump10 = jumps(1, 0, CHUNK, sides10)
         for a in range(GROUPS):
             for g in range(GROUPS):
                 quantise_w2(a, g, w2_bf[a, g])
+        jump10 = jumps(1, 0, CHUNK, sides10)
         sums_turned(0, 0, sides0, 0)
         sums_turned(1, 0, sides10, 0)
         for b in range(GROUPS):
@@ -348,16 +367,19 @@ def tile_list_face_jump_flux_kernel(
         magnitude(jump10)
         sides11 = pick(1, CHUNK, CHUNK)
         sums_direct(1, 1, sides11)
+        fluxes(0, 0)
         quantise_z(0, 1)
         quantise_z(1, 1)
         for g in range(GROUPS):
             products(g, 1)
         jump11 = jumps(1, CHUNK, CHUNK, sides11)
+        round_y(0, 0)
         magnitude(jump11)
-        for c in range(CHUNKS):
-            for g in range(GROUPS):
-                fluxes(g, c)
-                round_y(g, c)
+        fluxes(1, 0)
+        round_y(1, 0)
+        for g in range(GROUPS):
+            fluxes(g, 1)
+            round_y(g, 1)
         for c in range(CHUNKS):
             planes(c)
         store_scales()

from contextlib import ExitStack

import concourse.mybir as mybir
from concourse.masks import make_identity

K, H, T, S, NF = 1024, 1024, 4096, 1024, 512
FLOPS = 2 * K * H * S + 2 * H * H * NF

F32 = mybir.dt.float32
BF16 = mybir.dt.bfloat16
I32 = mybir.dt.int32
U32 = mybir.dt.uint32
U16 = mybir.dt.uint16
U8 = mybir.dt.uint8
FP8X4 = mybir.dt.float8_e4m3fn_x4
FP4X4 = mybir.dt.float4_e2m1fn_x4
ALU = mybir.AluOpType
ACT = mybir.ActivationFunctionType

P = 128
PACK = 4
GROUP = P * PACK
PASSES = K // GROUP
GROUPS = H // GROUP
BANK = 512
CHUNK = 256
CHUNKS = NF // CHUNK
BANKS = {(0, 0): 2, (1, 0): 6, (0, 1): 0, (1, 1): 4}
SUM_BANKS = {(0, 0): (0, 6), (1, 0): (2, 7), (0, 1): (0, 4)}
RUNS = ((0, 512), (512, 1024))
LAST_RUNS = ((0, 512), (512, 768), (768, 1024))
KIB = 1024
TAB0 = 0
GSC = 24 * KIB
TAB1 = 35 * KIB
PICKED = 52 * KIB
W2_RAW = {(0, 0): GSC + 256 - 8 * KIB, (0, 1): GSC + 768, (1, 0): TAB1, (1, 1): TAB1 + 9 * KIB}


def tile_list_face_jump_flux_kernel(
    tc, tab_words, tab_scales, offs, w1_words, w1_scales, pos1, pos2, w2, lam, out_0, out_1, out_2
):
    nc = tc.nc
    with ExitStack() as ctx:
        lists = ctx.enter_context(tc.tile_pool(name="lists", bufs=1))
        keep = ctx.enter_context(tc.tile_pool(name="keep", bufs=1))
        big = ctx.enter_context(tc.tile_pool(name="big", bufs=1))
        ring = ctx.enter_context(tc.tile_pool(name="ring", bufs=2))
        psum = ctx.enter_context(tc.psum_pool(name="psum", bufs=1))

        idx = lists.tile([P, S // 16], U16, name="idx")
        p1 = lists.tile([P, NF // 16], U16, name="p1")
        p2 = lists.tile([P, NF // 16], U16, name="p2")
        nc.sync.dma_start(idx[:], offs)

        tsc = big.tile([P, T], U8, name="tsc", align_bytes=64, offset=TAB1 - 2 * KIB)
        nc.sync.dma_start(tsc[0:32, :].bitcast(I32), tab_scales.rearrange("a q t -> (a q) t").bitcast(I32))

        w1sc_raw = keep.tile([P, PASSES, H], U8, name="w1sc_raw", align_bytes=64)
        nc.vector.memset(w1sc_raw[:].rearrange("p a n -> p (a n)").bitcast(I32), 0)
        nc.vector.memset(tsc[32:64, :].bitcast(I32), 0)
        nc.vector.memset(tsc[64:128, :].bitcast(I32), 0)
        vsc = [keep.tile([P, S], U8, name=f"vsc{a}", align_bytes=64) for a in range(PASSES)]
        for a in range(PASSES):
            nc.vector.memset(vsc[a][:].bitcast(I32), 0)

        tab = [big.tile([P, T], I32, name=f"tab{a}", offset=(TAB0, TAB1)[a]) for a in range(PASSES)]

        def load_words(a):
            nc.sync.dma_start(tab[a][:], tab_words[a].rearrange("p t i -> p (t i)").bitcast(I32))

        w1_raw = [
            keep.tile([P, PASSES, 2 * GROUP], U8, name="w1_raw0", align_bytes=64),
            big.tile([P, PASSES, 2 * GROUP], U8, name="w1_raw1", align_bytes=64, offset=TAB1 - 2 * KIB),
        ]

        def load_w1(b):
            nc.sync.dma_start(
                w1_raw[b][:].bitcast(I32),
                w1_words[:, :, 2 * GROUP * b : 2 * GROUP * (b + 1)].rearrange("a p n -> p a n").bitcast(I32),
            )

        nc.sync.dma_start(p1[:], pos1)
        nc.sync.dma_start(p2[:], pos2)
        lam_sb = keep.tile([P, GROUPS, PACK], F32, name="lam_sb")
        nc.sync.dma_start(lam_sb[:], lam.rearrange("(g p t) -> p g t", p=P, t=PACK))
        load_words(0)
        load_w1(0)

        for q in range(4):
            nc.gpsimd.dma_start(
                w1sc_raw[32 * q : 32 * q + 4, :, :].bitcast(I32),
                w1_scales[:, 4 * q : 4 * q + 4, :].rearrange("a r n -> r a n").bitcast(I32),
            )
        neg_lam = keep.tile([P, GROUPS, PACK], F32, name="neg_lam")
        nc.scalar.activation(out=neg_lam[:], in_=lam_sb[:], func=ACT.Copy, scale=-1.0)

        gsc = big.tile([P, S], U8, name="gsc", align_bytes=64, offset=GSC)
        nc.vector.tensor_copy(gsc[:], tsc[:].indirect(idx[:]))
        load_words(1)
        load_w1(1)
        for a in range(PASSES):
            for q in range(4):
                queue = nc.scalar if 4 * a + q < 6 else nc.gpsimd
                queue.dma_start(
                    vsc[a][32 * q : 32 * q + 4, :].bitcast(I32),
                    gsc[16 * a + 4 * q : 16 * a + 4 * q + 4, :].bitcast(I32),
                )

        ident = big.tile([P, P], F32, name="ident", offset=GSC + 256)
        make_identity(nc, ident[:])

        halves = S // BANK
        v = [
            [
                big.tile([P, BANK], U32, name=f"v{a}{s}", align_bytes=64, offset=PICKED + 2 * KIB * (halves * a + s))
                for s in range(halves)
            ]
            for a in range(PASSES)
        ]

        def gather_words(a):
            for j0, j1 in (LAST_RUNS if a == PASSES - 1 else RUNS):
                nc.vector.tensor_copy(
                    v[a][j0 // BANK][:, j0 % BANK : j0 % BANK + j1 - j0],
                    tab[a][:].bitcast(U32).indirect(idx[:, j0 // 16 : j1 // 16]),
                )

        gather_words(0)
        w1sc = {
            (b, a): big.tile(
                [P, GROUP], U8, name=f"w1sc{b}{a}", align_bytes=64,
                offset=TAB1 + 8 * KIB if (b, a) == (1, 1) else TAB0 + 12 * KIB + GROUP * (PASSES * b + a),
            )
            for b in range(GROUPS)
            for a in range(PASSES)
        }
        for (b, a), dealt in w1sc.items():
            if (b, a) == (1, 1):
                gather_words(1)
            nc.vector.tensor_copy(
                dealt[:].rearrange("p (t m) -> p t m", t=PACK),
                w1sc_raw[:, a, GROUP * b : GROUP * (b + 1)].rearrange("p (m t) -> p t m", t=PACK),
            )

        w1 = [keep.tile([P, PASSES, 2 * GROUP], U8, name=f"w1_{b}", align_bytes=64) for b in range(GROUPS)]
        for b in range(GROUPS):
            nc.scalar.copy(
                w1[b][:].bitcast(U16).rearrange("p a (t m) -> p a t m", t=PACK),
                w1_raw[b][:].bitcast(U16).rearrange("p a (m t) -> p a t m", t=PACK),
            )

        w2_raw = {}
        for a in range(GROUPS):
            for g in range(GROUPS):
                w2_raw[a, g] = big.tile([P, PACK, GROUP], F32, name=f"w2_raw{a}{g}", offset=W2_RAW[a, g])
                nc.sync.dma_start(
                    w2_raw[a, g][:],
                    w2[GROUP * a : GROUP * (a + 1), GROUP * g : GROUP * (g + 1)].rearrange("(p j) n -> p j n", j=PACK),
                )

        h = [keep.tile([P, S], F32, name=f"h{k}") for k in range(GROUPS * PACK)]
        steps = [
            (k, j0, j1) for k in range(GROUPS * PACK) for j0, j1 in (LAST_RUNS if k == 0 else RUNS)
        ]
        acc = {}
        for k, j0, j1 in steps:
            bank = 6 if (k, j0) == (0, 768) else (halves * k + j0 // BANK) % 6
            acc[k, j0] = psum.tile([P, j1 - j0], F32, name=f"acc{k}_{j0}", offset=2048 * bank)

        def states(k, j0, j1, a):
            b, t = divmod(k, PACK)
            nc.tensor.matmul_mx(
                out=acc[k, j0][:],
                lhsT=w1[b][:, a, 2 * P * t : 2 * P * (t + 1)].bitcast(FP4X4),
                lhsT_scale=w1sc[b, a][:, P * t : P * (t + 1)],
                rhs=v[a][j0 // BANK][:, j0 % BANK : j0 % BANK + j1 - j0].bitcast(FP8X4),
                rhs_scale=vsc[a][:, j0:j1],
                start=(a == 0),
                stop=(a == PASSES - 1),
            )

        early = [step for step in steps if step[0] < 3]
        for step in early:
            states(*step, 0)
        for step in steps:
            k, j0, j1 = step
            if step not in early:
                states(*step, 0)
            states(*step, 1)
            nc.scalar.copy(h[k][:, j0:j1], acc[k, j0][:])

        w2q = {}
        w2sc = {}

        def round_w2(a, g):
            w2_bf = keep.tile([P, PACK * GROUP], BF16, name=f"w2_bf{a}{g}", tag=f"stage{a}{g}", align_bytes=64)
            dst = w2_bf[:].rearrange("p (t m j) -> p m j t", t=PACK, j=PACK)
            src = w2_raw[a, g][:].rearrange("p j (m t) -> p m j t", t=PACK)
            if (a, g) in ():
                nc.vector.tensor_copy(dst, src)
            else:
                nc.scalar.copy(dst, src)
            return w2_bf

        def quantise_w2(a, g, w2_bf):
            w2q[a, g] = keep.tile([P, GROUP], U32, name=f"w2q{a}{g}", align_bytes=64)
            w2sc[a, g] = keep.tile([P, GROUP], U8, name=f"w2sc{a}{g}", align_bytes=64)
            nc.vector.quantize_mx(out=w2q[a, g][:].bitcast(FP8X4), scales=w2sc[a, g][:], in_=w2_bf[:])

        def pick(b, f0, width):
            last = b == 1 and f0 > 0
            side1 = keep.tile([P, PACK, width], F32, name=f"side1_{b}_{f0}", tag="stage11" if last else f"side1_{b}", align_bytes=64)
            side2 = keep.tile([P, PACK, width], F32, name=f"side2_{b}_{f0}", tag="zstage10" if last else f"side2_{b}", align_bytes=64)
            cols = slice(f0 // 16, (f0 + width) // 16)
            for t in range(PACK):
                nc.vector.tensor_copy(side1[:, t, :], h[PACK * b + t][:].indirect(p1[:, cols]))
                nc.vector.tensor_copy(side2[:, t, :], h[PACK * b + t][:].indirect(p2[:, cols]))
            return side1, side2

        jump = {}

        def jumps(b, f0, width, sides):
            if (b, f0) == (1, CHUNK):
                tile_j = keep.tile([P, PACK, width], F32, name=f"jump_{b}_{f0}")
            else:
                tile_j = big.tile([P, PACK, width], F32, name=f"jump_{b}_{f0}", offset=(PICKED, W2_RAW[0, 0])[b])
            nc.vector.tensor_tensor(tile_j[:], sides[0][:], sides[1][:], ALU.subtract)
            for c0 in range(0, width, CHUNK):
                jump[b, (f0 + c0) // CHUNK] = tile_j[:, :, c0 : c0 + CHUNK]
            return tile_j

        def magnitude(tile_j):
            per = BANK // tile_j.shape[2]
            for t in range(0, PACK, per):
                nc.scalar.activation(out=tile_j[:, t : t + per, :], in_=tile_j[:, t : t + per, :], func=ACT.Abs)

        z_bf = {}

        back = {}

        def new_z(b, c):
            z_bf[b, c] = keep.tile([P, CHUNK * PACK], BF16, name=f"z_bf{b}{c}", tag=f"zstage{b}{c}", align_bytes=64)
            return z_bf[b, c]

        def sums_turned(b, c, sides, c0):
            blocks = range(CHUNK // P)
            zt_bank, back_bank = SUM_BANKS[b, c]
            zt = [psum.tile([P, PACK, P], F32, name=f"zt{b}{c}{fb}", offset=2048 * (zt_bank + fb)) for fb in blocks]
            for t in range(PACK):
                for fb in blocks:
                    for side in range(2):
                        nc.tensor.matmul(
                            zt[fb][:, t, :], lhsT=sides[side][:, t, c0 + fb * P : c0 + (fb + 1) * P], rhs=ident[:],
                            is_transpose=True, start=(side == 0), stop=(side == 1),
                        )
            back[b, c] = psum.tile([P, CHUNK // P, 2, P], F32, name=f"back{b}{c}", offset=2048 * back_bank)
            for fb in blocks:
                zt_bf = keep.tile([P, 2, P, 2], BF16, name=f"zt_bf{b}{c}{fb}")
                nc.scalar.copy(zt_bf[:], zt[fb][:].rearrange("f (u e) p -> f u p e", e=2))
                words = zt_bf[:].rearrange("f u p e -> f (u p e)").bitcast(F32)
                for u in range(2):
                    nc.tensor.transpose(back[b, c][:, fb, u, :], words[:, u * P : (u + 1) * P], ident[:])

        def sums_back(b, c):
            nc.scalar.copy(
                new_z(b, c)[:].bitcast(F32).rearrange("p (fb f u) -> p fb f u", u=2, f=P),
                back[b, c][:].rearrange("p fb u f -> p fb f u"),
            )

        def sums_direct(b, c, sides):
            nc.vector.tensor_tensor(
                new_z(b, c)[:].rearrange("p (k i t) -> p k t i", i=2, t=PACK),
                sides[0][:].rearrange("p t (k i) -> p k t i", i=2),
                sides[1][:].rearrange("p t (k i) -> p k t i", i=2),
                ALU.add,
            )

        zq = {}
        zsc = {}

        def quantise_z(b, c):
            zq[b, c] = keep.tile([P, CHUNK], U32, name=f"zq{b}{c}", align_bytes=64)
            zsc[b, c] = keep.tile([P, CHUNK], U8, name=f"zsc{b}{c}", align_bytes=64)
            nc.vector.quantize_mx(out=zq[b, c][:].bitcast(FP8X4), scales=zsc[b, c][:], in_=z_bf[b, c][:])

        y = {}
        y_bf = {}
        ysc = keep.tile([P, GROUPS, NF], U8, name="ysc", align_bytes=64)
        out_rows = out_0.rearrange("(g p t) f -> g p t f", p=P, t=PACK)

        central = {}

        def products(g, c):
            per = BANK // CHUNK
            for t0 in range(0, PACK, per):
                bank = BANKS[g, c] + t0 // per
                acc = psum.tile([P, per, CHUNK], F32, name=f"central{g}{c}{t0}", offset=2048 * bank)
                for i in range(per):
                    cols = slice(P * (t0 + i), P * (t0 + i + 1))
                    central[g, c, t0 + i] = acc[:, i, :]
                    for a in reversed(range(GROUPS)):
                        nc.tensor.matmul_mx(
                            out=acc[:, i, :],
                            lhsT=w2q[a, g][:, cols].bitcast(FP8X4),
                            lhsT_scale=w2sc[a, g][:, cols],
                            rhs=zq[a, c][:].bitcast(FP8X4),
                            rhs_scale=zsc[a, c][:],
                            start=(a == GROUPS - 1),
                            stop=(a == 0),
                        )

        def fluxes(g, c):
            if (g, c) == (1, 1):
                y[g, c] = keep.tile([P, PACK, CHUNK], F32, name=f"y{g}{c}")
            else:
                y[g, c] = big.tile([P, PACK, CHUNK], F32, name=f"y{g}{c}", offset=TAB0 + 4 * KIB * (2 * c + g))
            for t in range(PACK):
                nc.vector.scalar_tensor_tensor(
                    y[g, c][:, t, :], jump[g, c][:, t, :], neg_lam[:, g, t : t + 1], central[g, c, t], ALU.mult, ALU.add
                )
            nc.sync.dma_start(out_rows[g, :, :, CHUNK * c : CHUNK * (c + 1)], y[g, c][:])

        def round_y(g, c):
            y_bf[g, c] = keep.tile([P, CHUNK * PACK], BF16, name=f"y_bf{g}{c}", align_bytes=64)
            nc.scalar.copy(
                y_bf[g, c][:].rearrange("p (k i t) -> p k t i", i=4, t=PACK),
                y[g, c][:].rearrange("p t (k i) -> p k t i", i=4),
            )

        def planes(c):
            yq = keep.tile([P, GROUPS, CHUNK], U32, name=f"yq{c}", align_bytes=64)
            for g in range(GROUPS):
                nc.vector.quantize_mx(
                    out=yq[:, g, :].bitcast(FP8X4), scales=ysc[:, g, CHUNK * c : CHUNK * (c + 1)], in_=y_bf[g, c][:]
                )
            nc.sync.dma_start(
                out_1[:, :, CHUNK * c : CHUNK * (c + 1), :].rearrange("g p m t -> p g (m t)").bitcast(I32),
                yq[:].bitcast(I32),
            )

        def store_scales():
            for q in range(4):
                (nc.scalar, nc.sync)[q % 2].dma_start(
                    out_2[:, 4 * q : 4 * q + 4, :].rearrange("g r m -> r g m").bitcast(I32),
                    ysc[32 * q : 32 * q + 4, :, :].bitcast(I32),
                )

        w2_bf = {(a, g): round_w2(a, g) for a in range(GROUPS) for g in range(GROUPS)}
        sides0 = pick(0, 0, NF)
        jump0 = jumps(0, 0, NF, sides0)
        sides10 = pick(1, 0, CHUNK)
        for a in range(GROUPS):
            for g in range(GROUPS):
                quantise_w2(a, g, w2_bf[a, g])
        jump10 = jumps(1, 0, CHUNK, sides10)
        sums_turned(0, 0, sides0, 0)
        sums_turned(1, 0, sides10, 0)
        for b in range(GROUPS):
            sums_back(b, 0)
            quantise_z(b, 0)
        sums_turned(0, 1, sides0, CHUNK)
        sums_back(0, 1)
        for g in range(GROUPS):
            products(g, 0)
        magnitude(jump0)
        magnitude(jump10)
        sides11 = pick(1, CHUNK, CHUNK)
        sums_direct(1, 1, sides11)
        fluxes(0, 0)
        quantise_z(0, 1)
        quantise_z(1, 1)
        for g in range(GROUPS):
            products(g, 1)
        jump11 = jumps(1, CHUNK, CHUNK, sides11)
        round_y(0, 0)
        magnitude(jump11)
        fluxes(1, 0)
        round_y(1, 0)
        for g in range(GROUPS):
            fluxes(g, 1)
            round_y(g, 1)
        for c in range(CHUNKS):
            planes(c)
        store_scales()
